import numpy as np
import ml_dtypes


def mxq(x, axis, fmt="e4m3"):
    dtype, down = {"e4m3": (ml_dtypes.float8_e4m3fn, 7), "e5m2": (ml_dtypes.float8_e5m2, 14)}[fmt]
    v = np.moveaxis(np.asarray(x, np.float32).astype(ml_dtypes.bfloat16).astype(np.float64), axis, -1)
    blocks = v.reshape(v.shape[:-1] + (-1, 32))
    amax = np.abs(blocks).max(-1, keepdims=True)
    byte = np.maximum(np.where(amax > 0, np.frexp(amax)[1] - 1 + 127, 0) - down, 1)
    scale = np.exp2(byte - 127.0)
    codes = (blocks / scale).astype(np.float32).astype(dtype).astype(np.float64)
    return np.moveaxis((codes * scale).reshape(v.shape), -1, axis)


WIDE = False


def mx_kscale(k):
    if not WIDE:
        return np.ones(k)
    levels = np.array([10, -10, 5, -5, 0])
    if k % 512:
        return np.exp2(np.random.permutation(np.resize(levels, k // 32))).repeat(32)
    a = np.empty((k // 512, 16))
    for p in range(k // 512):
        a[p, :8] = np.random.permutation(np.resize(levels, 8))
        for g in range(8):
            far = levels[np.abs(levels - a[p, g]) >= 10]
            a[p, g + 8] = far[np.random.randint(len(far))]
    return np.exp2(a.ravel()).repeat(32)


def f64(x):
    return np.asarray(x).astype(np.float64)


def striped(idx):
    return np.tile(idx.reshape(-1, 16).T, (8, 1)).astype(np.uint16)


def unstriped(offs):
    return offs[:16].T.reshape(-1).astype(np.int64)


E2M1 = np.array([0.0, 0.5, 1.0, 1.5, 2.0, 3.0, 4.0, 6.0, -0.0, -0.5, -1.0, -1.5, -2.0, -3.0, -4.0, -6.0])


def pack_weight(w, fmt):
    k, n = w.shape
    w = f64(np.asarray(w, np.float32).astype(ml_dtypes.bfloat16)).reshape(k // 32, 32, n)
    amax = np.abs(w).max(1)
    if fmt == "e4m3":
        byte = np.frexp(amax)[1] - 1 + 127 - 7
    else:
        mant, ex = np.frexp(amax / 6.0)
        byte = np.where(mant > 0.5, ex, ex - 1) + 127
    byte = np.clip(np.where(amax > 0, byte, 1), 1, 254)
    scaled = (w * np.exp2(127.0 - byte)[:, None, :]).reshape(k, n).astype(np.float32)
    by_word = np.ascontiguousarray(scaled.reshape(k // 512, 128, 4, n).transpose(0, 1, 3, 2))
    if fmt == "e4m3":
        words = by_word.astype(ml_dtypes.float8_e4m3fn).view(np.uint8)
    else:
        c = by_word.astype(ml_dtypes.float4_e2m1fn).view(np.uint8) & 0xF
        words = (c[..., 0::2] | (c[..., 1::2] << 4)).reshape(k // 512, 128, 2 * n)
    return np.ascontiguousarray(words), np.ascontiguousarray(byte.astype(np.uint8).reshape(k // 512, 16, n))


def unpack_weight(words, scales, fmt):
    g, _, n = scales.shape
    words = np.ascontiguousarray(words).reshape(g, 128, n, -1)
    if fmt == "e4m3":
        vals = words.view(ml_dtypes.float8_e4m3fn).astype(np.float64)
    else:
        nib = np.empty((g, 128, n, 4), np.uint8)
        nib[..., 0::2] = words & 0xF
        nib[..., 1::2] = words >> 4
        vals = E2M1[nib]
    vals = vals * np.repeat(np.exp2(scales.astype(np.float64) - 127.0), 8, axis=1)[..., None]
    return vals.transpose(0, 1, 3, 2).reshape(g * 512, n)


def gelu(v):
    return 0.5 * v * (1.0 + np.tanh(np.sqrt(2.0 / np.pi) * (v + 0.044715 * v**3)))


K, H, N, T, S = 1024, 1024, 512, 4096, 512

def setup_inputs():
    n = np.random.standard_normal
    s = mx_kscale(K)[:, None]
    u = mx_kscale(H)[:, None]
    tab_words, tab_scales = pack_weight(n((K, T)) * s, "e4m3")
    w1_words, w1_scales = pack_weight(n((K, H)) / np.sqrt(K) / s * u.T, "e2m1")
    return {
        "tab_words": tab_words,
        "tab_scales": tab_scales,
        "w1_words": w1_words,
        "w1_scales": w1_scales,
        "w2": (n((H, N)) / np.sqrt(H) / u).astype(np.float32),
        "b2": (0.8 * n(N)).astype(np.float32),
        "offs": striped(np.random.permutation(T)[:S]),
        "offs2": striped(np.random.permutation(T)[:S]),
        "offs3": striped(np.random.permutation(T)[:S]),
    }

def reference(tab_words, tab_scales, w1_words, w1_scales, w2, b2, offs, offs2, offs3):
    TW = unpack_weight(tab_words, tab_scales, "e4m3")
    v = TW[:, unstriped(offs)]
    v2 = TW[:, unstriped(offs2)]
    v3 = TW[:, unstriped(offs3)]
    w1 = unpack_weight(w1_words, w1_scales, "e2m1")
    post = w1.T @ v
    copy = w1.T @ v2
    press = w1.T @ v3
    h = np.maximum(np.abs(post - copy), np.abs(copy - press))
    y = mxq(f64(w2), 0, "e4m3").T @ mxq(h, 0, "e4m3")
    return y + f64(b2)[:, None]

@@ -1,0 +1,243 @@
+from contextlib import ExitStack
+
+import concourse.mybir as mybir
+
+K, H, N, T, S = 1024, 1024, 512, 4096, 512
+FLOPS = 2 * (3 * K * H * S + H * N * S)
+
+F32 = mybir.dt.float32
+BF16 = mybir.dt.bfloat16
+I32 = mybir.dt.int32
+U32 = mybir.dt.uint32
+U16 = mybir.dt.uint16
+U8 = mybir.dt.uint8
+FP8X4 = mybir.dt.float8_e4m3fn_x4
+FP4X4 = mybir.dt.float4_e2m1fn_x4
+ALU = mybir.AluOpType
+ACT = mybir.ActivationFunctionType
+
+P = 128
+PACK = 4
+K_PASS = P * PACK
+K_PASSES = K // K_PASS
+H_PASSES = H // K_PASS
+RUN = 8
+BLOCKS = K_PASS // 32
+QUADS = 4
+HALF = S // 2
+POST, COPY, PRESS = 0, 1, 2
+LIST_ORDER = (COPY, POST, PRESS)
+
+
+def tile_list_rumour_distortion_scores_kernel(
+    tc, tab_words, tab_scales, w1_words, w1_scales, w2, b2, offs, offs2, offs3, out
+):
+    nc = tc.nc
+    with ExitStack() as ctx:
+        keep = ctx.enter_context(tc.tile_pool(name="keep", bufs=1))
+        work = ctx.enter_context(tc.tile_pool(name="work", bufs=2))
+        psum = ctx.enter_context(tc.psum_pool(name="psum", bufs=8))
+
+        scale_window = keep.tile([P, T], U8, name="scale_window", align_bytes=64)
+        nc.sync.dma_start(
+            out=scale_window[0:32, :].bitcast(I32),
+            in_=tab_scales.rearrange("a q t -> (a q) t").bitcast(I32),
+        )
+        nc.vector.memset(scale_window[32:64, :].bitcast(I32), 0)
+        nc.vector.memset(scale_window[64:128, :].bitcast(I32), 0)
+
+        list_inputs = (offs, offs2, offs3)
+        lists = {}
+        for l in LIST_ORDER:
+            lists[l] = keep.tile([P, S // 16], U16, name="list%d" % l)
+            nc.sync.dma_start(lists[l][:], list_inputs[l])
+
+        def load_table(a):
+            window = keep.tile([P, T], U32, name="word_window%d" % a, align_bytes=64)
+            nc.sync.dma_start(
+                out=window[:].bitcast(I32),
+                in_=tab_words[a].rearrange("p t i -> p (t i)").bitcast(I32),
+            )
+            return window
+
+        def load_w1(b, tag, engine):
+            raw = keep.tile([P, K_PASSES, 2 * K_PASS], U8, name="w1_raw%d" % b, tag=tag, align_bytes=64)
+            nc.sync.dma_start(
+                out=raw[:].bitcast(I32),
+                in_=w1_words[:, :, 2 * K_PASS * b : 2 * K_PASS * (b + 1)].rearrange("a p c -> p a c").bitcast(I32),
+            )
+            dealt = keep.tile([P, K_PASSES, PACK, 2 * P], U8, name="w1_dealt%d" % b, align_bytes=64)
+            engine.tensor_copy(
+                out=dealt[:].bitcast(I32).rearrange("p a t (g w) -> p a t g w", g=BLOCKS),
+                in_=raw[:].bitcast(I32).rearrange("p a (g t w) -> p a t g w", g=BLOCKS, t=PACK),
+            )
+            return dealt
+
+        word_windows = [load_table(0)]
+        w1_codes = [load_w1(0, "w1_then_w2", nc.vector)]
+        word_windows.append(load_table(1))
+
+        w1_scale_raw = keep.tile([P, K_PASSES * H], U8, name="w1_scale_raw", align_bytes=64)
+        nc.gpsimd.memset(w1_scale_raw[:].bitcast(I32), 0)
+        for r in range(4):
+            nc.gpsimd.dma_start(
+                out=w1_scale_raw[r:P:32, :].bitcast(I32).rearrange("q (a c) -> q a c", a=K_PASSES),
+                in_=w1_scales.bitcast(I32)[:, r:BLOCKS:4, :].rearrange("a q c -> q a c"),
+            )
+        bias = keep.tile([P, N // P], F32, name="bias")
+        with nc.allow_non_contiguous_dma(reason="one bias value a partition"):
+            nc.gpsimd.dma_start(out=bias[:], in_=b2.rearrange("(m p) -> p m", p=P))
+        w1_scale = keep.tile([P, K_PASSES * H], U8, name="w1_scale", align_bytes=64)
+        nc.gpsimd.tensor_copy(
+            out=w1_scale[:].bitcast(I32).rearrange("p (x t g w) -> p x t g w", t=PACK, g=BLOCKS, w=2),
+            in_=w1_scale_raw[:].bitcast(I32).rearrange("p (x g t w) -> p x t g w", t=PACK, g=BLOCKS, w=2),
+        )
+
+        planes = []
+        for a in range(K_PASSES):
+            plane = keep.tile([P, 3 * S], U8, name="plane%d" % a, align_bytes=64)
+            nc.gpsimd.memset(plane[:].bitcast(I32), 0)
+            planes.append(plane)
+        picked_scales = keep.tile([P, 3 * S], U8, name="picked_scales", tag="picked_then_w1", align_bytes=64)
+        for l in LIST_ORDER:
+            nc.vector.tensor_copy(picked_scales[:, l * S : (l + 1) * S], scale_window[:].indirect(lists[l][:]))
+        for a in range(K_PASSES):
+            for q in range(QUADS):
+                last = a == K_PASSES - 1 and q == QUADS - 1
+                queue = nc.gpsimd if last else nc.scalar
+                row = BLOCKS * a + 4 * q
+                queue.dma_start(
+                    out=planes[a][32 * q : 32 * q + 4, :].bitcast(I32),
+                    in_=picked_scales[row : row + 4, :].bitcast(I32),
+                )
+
+        picked = {}
+        for a in range(K_PASSES):
+            for l in LIST_ORDER:
+                picked[l, a] = keep.tile([P, S], U32, name="picked%d_%d" % (l, a), align_bytes=64)
+        for l in LIST_ORDER:
+            nc.vector.tensor_copy(picked[l, 0][:], word_windows[0][:].indirect(lists[l][:]))
+        for h in range(2):
+            for l in LIST_ORDER:
+                nc.vector.tensor_copy(
+                    picked[l, 1][:, h * HALF : (h + 1) * HALF],
+                    word_windows[1][:].indirect(lists[l][:, h * 16 : (h + 1) * 16]),
+                )
+
+        w1_codes.append(load_w1(1, "picked_then_w1", nc.gpsimd))
+        w2_raw = keep.tile([P, H_PASSES * PACK * N], F32, name="w2_raw", tag="w1_then_w2", align_bytes=64)
+
+        w2_codes = []
+        w2_scales = []
+        for b in range(H_PASSES):
+            rows = w2[K_PASS * b : K_PASS * (b + 1), :].rearrange("(g t i) n -> t g i n", g=BLOCKS, t=PACK)
+            raw = w2_raw[:, b * PACK * N : (b + 1) * PACK * N].rearrange("p (t n) -> p t n", t=PACK)
+            for t in range(PACK):
+                nc.sync.dma_start(out=raw[:, t, :], in_=rows[t])
+            grouped = keep.tile([P, N, PACK], BF16, name="w2_grouped%d" % b, align_bytes=64)
+            for m in range(N // P):
+                cols = slice(m * P, (m + 1) * P)
+                nc.gpsimd.tensor_copy(out=grouped[:, cols, :], in_=raw[:, :, cols].rearrange("p t n -> p n t"))
+            codes = keep.tile([P, N], U32, name="w2_codes%d" % b, align_bytes=64)
+            scales = keep.tile([P, N], U8, name="w2_scales%d" % b, align_bytes=64)
+            w2_codes.append(codes)
+            w2_scales.append((scales, grouped))
+
+        def quantize_w2(b):
+            scales, grouped = w2_scales[b]
+            nc.vector.quantize_mx(
+                out=w2_codes[b][:].bitcast(FP8X4),
+                scales=scales[:],
+                in_=grouped[:].rearrange("p n t -> p (n t)"),
+            )
+
+        h_codes = {}
+        h_scales = {}
+
+        def first_stage(b, h):
+            cols = slice(h * HALF, (h + 1) * HALF)
+            gaps = work.tile([P, 2, PACK, HALF], F32, name="gaps")
+            for pair in range(PACK // 2):
+                sums = {}
+                for l in LIST_ORDER:
+                    sums[l] = psum.tile([P, 2 * HALF], F32, name="bank")
+                    for a in range(K_PASSES):
+                        for u in range(2):
+                            t = 2 * pair + u
+                            w_col = a * H + b * K_PASS + t * P
+                            nc.tensor.matmul_mx(
+                                out=sums[l][:, u * HALF : (u + 1) * HALF],
+                                lhsT=w1_codes[b][:, a, t, :].bitcast(FP4X4),
+                                lhsT_scale=w1_scale[:, w_col : w_col + P],
+                                rhs=picked[l, a][:, cols].bitcast(FP8X4),
+                                rhs_scale=planes[a][:, l * S + h * HALF : l * S + (h + 1) * HALF],
+                                start=(a == 0 and u == 0),
+                                stop=(a == K_PASSES - 1 and u == 1),
+                            )
+                copy_sums = work.tile([P, 2 * HALF], F32, name="copy_sums", bufs=3)
+                nc.scalar.copy(out=copy_sums[:], in_=sums[COPY][:])
+                diffs = work.tile([P, 2, 2 * HALF], F32, name="diffs", bufs=3)
+                nc.vector.tensor_tensor(diffs[:, 0, :], sums[POST][:], copy_sums[:], ALU.subtract)
+                nc.vector.tensor_tensor(diffs[:, 1, :], sums[PRESS][:], copy_sums[:], ALU.subtract)
+                nc.scalar.activation(
+                    out=gaps[:, :, 2 * pair : 2 * pair + 2, :].rearrange("p d t j -> p d (t j)"),
+                    in_=diffs[:],
+                    func=ACT.Abs,
+                )
+            grouped = work.tile([P, HALF, PACK], BF16, name="h_grouped", align_bytes=64)
+            nc.vector.tensor_tensor(
+                grouped[:].rearrange("p (c i) t -> p c t i", i=4),
+                gaps[:, 0].rearrange("p t (c i) -> p c t i", i=4),
+                gaps[:, 1].rearrange("p t (c i) -> p c t i", i=4),
+                ALU.max,
+            )
+            h_codes[b, h] = keep.tile([P, HALF], U32, name="h_codes%d_%d" % (b, h), align_bytes=64)
+            h_scales[b, h] = keep.tile([P, HALF], U8, name="h_scales%d_%d" % (b, h), align_bytes=64)
+            nc.vector.quantize_mx(
+                out=h_codes[b, h][:].bitcast(FP8X4),
+                scales=h_scales[b, h][:],
+                in_=grouped[:].rearrange("p j t -> p (j t)"),
+            )
+
+        out_rows = out.rearrange("(m p) j -> p m j", p=P)
+
+        def second_stage(h):
+            cols = slice(h * HALF, (h + 1) * HALF)
+            for pair in range(2):
+                acc = psum.tile([P, 2 * HALF], F32, name="bank")
+                for b in range(H_PASSES):
+                    for u in range(2):
+                        m = 2 * pair + u
+                        nc.tensor.matmul_mx(
+                            out=acc[:, u * HALF : (u + 1) * HALF],
+                            lhsT=w2_codes[b][:, m * P : (m + 1) * P].bitcast(FP8X4),
+                            lhsT_scale=w2_scales[b][0][:, m * P : (m + 1) * P],
+                            rhs=h_codes[b, h][:].bitcast(FP8X4),
+                            rhs_scale=h_scales[b, h][:],
+                            start=(b == 0 and u == 0),
+                            stop=(b == H_PASSES - 1 and u == 1),
+                        )
+                result = work.tile([P, 2, HALF], F32, name="result", bufs=4)
+                for u in range(2):
+                    m = 2 * pair + u
+                    if h == 1 and pair == 1:
+                        nc.vector.tensor_scalar(
+                            result[:, u, :], acc[:, u * HALF : (u + 1) * HALF], bias[:, m : m + 1], None, ALU.add
+                        )
+                    else:
+                        nc.scalar.activation(
+                            out=result[:, u, :],
+                            in_=acc[:, u * HALF : (u + 1) * HALF],
+                            func=ACT.Identity,
+                            bias=bias[:, m : m + 1],
+                        )
+                nc.sync.dma_start(out=out_rows[:, 2 * pair : 2 * pair + 2, cols], in_=result[:])
+
+        first_stage(0, 0)
+        first_stage(0, 1)
+        quantize_w2(0)
+        first_stage(1, 0)
+        quantize_w2(1)
+        second_stage(0)
+        first_stage(1, 1)
+        second_stage(1)

@@ -25,6 +25,7 @@ RUN = 8
 BLOCKS = K_PASS // 32
 QUADS = 4
 HALF = S // 2
+W1_COL = 3 * S
 POST, COPY, PRESS = 0, 1, 2
 LIST_ORDER = (COPY, POST, PRESS)
 
@@ -46,6 +47,14 @@ def tile_list_rumour_distortion_scores_kernel(
         nc.vector.memset(scale_window[32:64, :].bitcast(I32), 0)
         nc.vector.memset(scale_window[64:128, :].bitcast(I32), 0)
 
+        w1_scale_raw = keep.tile([P, H], U8, name="w1_scale_raw", align_bytes=64)
+        nc.sync.dma_start(
+            out=w1_scale_raw[0:32, :].bitcast(I32),
+            in_=w1_scales.rearrange("a q c -> (a q) c").bitcast(I32),
+        )
+        nc.gpsimd.memset(w1_scale_raw[32:64, :].bitcast(I32), 0)
+        nc.gpsimd.memset(w1_scale_raw[64:128, :].bitcast(I32), 0)
+
         list_inputs = (offs, offs2, offs3)
         lists = {}
         for l in LIST_ORDER:
@@ -53,63 +62,50 @@ def tile_list_rumour_distortion_scores_kernel(
             nc.sync.dma_start(lists[l][:], list_inputs[l])
 
         def load_table(a):
-            window = keep.tile([P, T], U32, name="word_window%d" % a, align_bytes=64)
+            window = keep.tile([P, T], U32, name="word_window%d" % a, tag="table%d" % a, align_bytes=64)
             nc.sync.dma_start(
                 out=window[:].bitcast(I32),
                 in_=tab_words[a].rearrange("p t i -> p (t i)").bitcast(I32),
             )
             return window
 
-        def load_w1(b, tag, engine):
+        def load_w1(b, tag):
             raw = keep.tile([P, K_PASSES, 2 * K_PASS], U8, name="w1_raw%d" % b, tag=tag, align_bytes=64)
             nc.sync.dma_start(
                 out=raw[:].bitcast(I32),
                 in_=w1_words[:, :, 2 * K_PASS * b : 2 * K_PASS * (b + 1)].rearrange("a p c -> p a c").bitcast(I32),
             )
             dealt = keep.tile([P, K_PASSES, PACK, 2 * P], U8, name="w1_dealt%d" % b, align_bytes=64)
-            engine.tensor_copy(
-                out=dealt[:].bitcast(I32).rearrange("p a t (g w) -> p a t g w", g=BLOCKS),
-                in_=raw[:].bitcast(I32).rearrange("p a (g t w) -> p a t g w", g=BLOCKS, t=PACK),
+            nc.scalar.copy(
+                out=dealt[:].bitcast(U32).rearrange("p a t (g w) -> p a t g w", g=BLOCKS),
+                in_=raw[:].bitcast(U32).rearrange("p a (g t w) -> p a t g w", g=BLOCKS, t=PACK),
             )
             return dealt
 
         word_windows = [load_table(0)]
-        w1_codes = [load_w1(0, "w1_then_w2", nc.vector)]
+        w1_codes = [load_w1(0, "w1_then_w2")]
         word_windows.append(load_table(1))
-
-        w1_scale_raw = keep.tile([P, K_PASSES * H], U8, name="w1_scale_raw", align_bytes=64)
-        nc.gpsimd.memset(w1_scale_raw[:].bitcast(I32), 0)
-        for r in range(4):
-            nc.gpsimd.dma_start(
-                out=w1_scale_raw[r:P:32, :].bitcast(I32).rearrange("q (a c) -> q a c", a=K_PASSES),
-                in_=w1_scales.bitcast(I32)[:, r:BLOCKS:4, :].rearrange("a q c -> q a c"),
-            )
-        bias = keep.tile([P, N // P], F32, name="bias")
-        with nc.allow_non_contiguous_dma(reason="one bias value a partition"):
-            nc.gpsimd.dma_start(out=bias[:], in_=b2.rearrange("(m p) -> p m", p=P))
-        w1_scale = keep.tile([P, K_PASSES * H], U8, name="w1_scale", align_bytes=64)
-        nc.gpsimd.tensor_copy(
-            out=w1_scale[:].bitcast(I32).rearrange("p (x t g w) -> p x t g w", t=PACK, g=BLOCKS, w=2),
-            in_=w1_scale_raw[:].bitcast(I32).rearrange("p (x g t w) -> p x t g w", t=PACK, g=BLOCKS, w=2),
-        )
 
         planes = []
         for a in range(K_PASSES):
-            plane = keep.tile([P, 3 * S], U8, name="plane%d" % a, align_bytes=64)
-            nc.gpsimd.memset(plane[:].bitcast(I32), 0)
-            planes.append(plane)
-        picked_scales = keep.tile([P, 3 * S], U8, name="picked_scales", tag="picked_then_w1", align_bytes=64)
+            planes.append(keep.tile([P, W1_COL + H], U8, name="plane%d" % a, align_bytes=64))
+        nc.gpsimd.memset(planes[1][:].bitcast(I32), 0)
+        nc.scalar.copy(
+            out=planes[0][:, W1_COL:].bitcast(U32).rearrange("p (b t g w) -> p b t g w", t=PACK, g=BLOCKS, w=2),
+            in_=w1_scale_raw[:].bitcast(U32).rearrange("p (b g t w) -> p b t g w", t=PACK, g=BLOCKS, w=2),
+        )
+        picked_scales = keep.tile([P, 3 * S], U8, name="picked_scales", align_bytes=64)
         for l in LIST_ORDER:
             nc.vector.tensor_copy(picked_scales[:, l * S : (l + 1) * S], scale_window[:].indirect(lists[l][:]))
+        nc.vector.tensor_copy(planes[0][:, 0:W1_COL].bitcast(I32), picked_scales[:].bitcast(I32))
         for a in range(K_PASSES):
             for q in range(QUADS):
-                last = a == K_PASSES - 1 and q == QUADS - 1
-                queue = nc.gpsimd if last else nc.scalar
-                row = BLOCKS * a + 4 * q
-                queue.dma_start(
-                    out=planes[a][32 * q : 32 * q + 4, :].bitcast(I32),
-                    in_=picked_scales[row : row + 4, :].bitcast(I32),
-                )
+                if a + q > 0:
+                    row = BLOCKS * a + 4 * q
+                    nc.scalar.dma_start(
+                        out=planes[a][32 * q : 32 * q + 4, :].bitcast(I32),
+                        in_=planes[0][row : row + 4, :].bitcast(I32),
+                    )
 
         picked = {}
         for a in range(K_PASSES):
@@ -124,8 +120,9 @@ def tile_list_rumour_distortion_scores_kernel(
                     word_windows[1][:].indirect(lists[l][:, h * 16 : (h + 1) * 16]),
                 )
 
-        w1_codes.append(load_w1(1, "picked_then_w1", nc.gpsimd))
-        w2_raw = keep.tile([P, H_PASSES * PACK * N], F32, name="w2_raw", tag="w1_then_w2", align_bytes=64)
+        w1_codes.append(load_w1(1, "table0"))
+        w2_raw = keep.tile([P, H_PASSES * PACK * N + N // P], F32, name="w2_raw", tag="w1_then_w2", align_bytes=64)
+        bias = w2_raw[:, H_PASSES * PACK * N :]
 
         w2_codes = []
         w2_scales = []
@@ -137,11 +134,16 @@ def tile_list_rumour_distortion_scores_kernel(
             grouped = keep.tile([P, N, PACK], BF16, name="w2_grouped%d" % b, align_bytes=64)
             for m in range(N // P):
                 cols = slice(m * P, (m + 1) * P)
-                nc.gpsimd.tensor_copy(out=grouped[:, cols, :], in_=raw[:, :, cols].rearrange("p t n -> p n t"))
+                nc.gpsimd.tensor_scalar(
+                    grouped[:, cols, :], raw[:, :, cols].rearrange("p t n -> p n t"), 1.0, 0.0, ALU.mult, ALU.add
+                )
             codes = keep.tile([P, N], U32, name="w2_codes%d" % b, align_bytes=64)
             scales = keep.tile([P, N], U8, name="w2_scales%d" % b, align_bytes=64)
             w2_codes.append(codes)
             w2_scales.append((scales, grouped))
+
+        with nc.allow_non_contiguous_dma(reason="one bias value a partition"):
+            nc.sync.dma_start(out=bias, in_=b2.rearrange("(m p) -> p m", p=P))
 
         def quantize_w2(b):
             scales, grouped = w2_scales[b]
@@ -164,11 +166,11 @@ def tile_list_rumour_distortion_scores_kernel(
                     for a in range(K_PASSES):
                         for u in range(2):
                             t = 2 * pair + u
-                            w_col = a * H + b * K_PASS + t * P
+                            w_col = W1_COL + b * K_PASS + t * P
                             nc.tensor.matmul_mx(
                                 out=sums[l][:, u * HALF : (u + 1) * HALF],
                                 lhsT=w1_codes[b][:, a, t, :].bitcast(FP4X4),
-                                lhsT_scale=w1_scale[:, w_col : w_col + P],
+                                lhsT_scale=planes[a][:, w_col : w_col + P],
                                 rhs=picked[l, a][:, cols].bitcast(FP8X4),
                                 rhs_scale=planes[a][:, l * S + h * HALF : l * S + (h + 1) * HALF],
                                 start=(a == 0 and u == 0),

@@ -26,6 +26,7 @@ BLOCKS = K_PASS // 32
 QUADS = 4
 HALF = S // 2
 W1_COL = 3 * S
+BANK = 512
 POST, COPY, PRESS = 0, 1, 2
 LIST_ORDER = (COPY, POST, PRESS)
 
@@ -153,93 +154,86 @@ def tile_list_rumour_distortion_scores_kernel(
                 in_=grouped[:].rearrange("p n t -> p (n t)"),
             )
 
-        h_codes = {}
-        h_scales = {}
+        h_codes = []
+        h_scales = []
+        for b in range(H_PASSES):
+            h_codes.append(keep.tile([P, S], U32, name="h_codes%d" % b, align_bytes=64))
+            h_scales.append(keep.tile([P, S], U8, name="h_scales%d" % b, align_bytes=64))
 
-        def first_stage(b, h):
-            cols = slice(h * HALF, (h + 1) * HALF)
-            gaps = work.tile([P, 2, PACK, HALF], F32, name="gaps")
-            for pair in range(PACK // 2):
+        def first_stage(b, j0, width):
+            cols = slice(j0, j0 + width)
+            per_bank = BANK // width
+            groups = PACK // per_bank
+            gaps = work.tile([P, 2, groups, BANK], F32, name="gaps")
+            for q in range(groups):
                 sums = {}
                 for l in LIST_ORDER:
-                    sums[l] = psum.tile([P, 2 * HALF], F32, name="bank")
+                    bank = psum.tile([P, BANK], F32, name="bank", bufs=6)
                     for a in range(K_PASSES):
-                        for u in range(2):
-                            t = 2 * pair + u
+                        for u in range(per_bank):
+                            t = per_bank * q + u
                             w_col = W1_COL + b * K_PASS + t * P
                             nc.tensor.matmul_mx(
-                                out=sums[l][:, u * HALF : (u + 1) * HALF],
+                                out=bank[:, u * width : (u + 1) * width],
                                 lhsT=w1_codes[b][:, a, t, :].bitcast(FP4X4),
                                 lhsT_scale=planes[a][:, w_col : w_col + P],
                                 rhs=picked[l, a][:, cols].bitcast(FP8X4),
-                                rhs_scale=planes[a][:, l * S + h * HALF : l * S + (h + 1) * HALF],
+                                rhs_scale=planes[a][:, l * S + j0 : l * S + j0 + width],
                                 start=(a == 0 and u == 0),
-                                stop=(a == K_PASSES - 1 and u == 1),
+                                stop=(a == K_PASSES - 1 and u == per_bank - 1),
                             )
-                copy_sums = work.tile([P, 2 * HALF], F32, name="copy_sums", bufs=3)
-                nc.scalar.copy(out=copy_sums[:], in_=sums[COPY][:])
-                diffs = work.tile([P, 2, 2 * HALF], F32, name="diffs", bufs=3)
-                nc.vector.tensor_tensor(diffs[:, 0, :], sums[POST][:], copy_sums[:], ALU.subtract)
-                nc.vector.tensor_tensor(diffs[:, 1, :], sums[PRESS][:], copy_sums[:], ALU.subtract)
+                    sums[l] = bank[:].rearrange("p (u j) -> p j u", u=per_bank)
+                copy_sums = work.tile([P, width, per_bank], F32, name="copy_sums", bufs=3)
+                nc.scalar.copy(out=copy_sums[:], in_=sums[COPY])
+                diffs = work.tile([P, 2, width, per_bank], F32, name="diffs", bufs=3)
+                nc.vector.tensor_tensor(diffs[:, 0], sums[POST], copy_sums[:], ALU.subtract)
+                nc.vector.tensor_tensor(diffs[:, 1], sums[PRESS], copy_sums[:], ALU.subtract)
                 nc.scalar.activation(
-                    out=gaps[:, :, 2 * pair : 2 * pair + 2, :].rearrange("p d t j -> p d (t j)"),
-                    in_=diffs[:],
-                    func=ACT.Abs,
+                    out=gaps[:, :, q, :], in_=diffs[:].rearrange("p d j u -> p d (j u)"), func=ACT.Abs
                 )
-            grouped = work.tile([P, HALF, PACK], BF16, name="h_grouped", align_bytes=64)
+            grouped = work.tile([P, width * PACK], BF16, name="h_grouped", align_bytes=64)
             nc.vector.tensor_tensor(
-                grouped[:].rearrange("p (c i) t -> p c t i", i=4),
-                gaps[:, 0].rearrange("p t (c i) -> p c t i", i=4),
-                gaps[:, 1].rearrange("p t (c i) -> p c t i", i=4),
+                grouped[:].rearrange("p (j q u) -> p j q u", q=groups, u=per_bank),
+                gaps[:, 0].rearrange("p q (j u) -> p j q u", u=per_bank),
+                gaps[:, 1].rearrange("p q (j u) -> p j q u", u=per_bank),
                 ALU.max,
             )
-            h_codes[b, h] = keep.tile([P, HALF], U32, name="h_codes%d_%d" % (b, h), align_bytes=64)
-            h_scales[b, h] = keep.tile([P, HALF], U8, name="h_scales%d_%d" % (b, h), align_bytes=64)
-            nc.vector.quantize_mx(
-                out=h_codes[b, h][:].bitcast(FP8X4),
-                scales=h_scales[b, h][:],
-                in_=grouped[:].rearrange("p j t -> p (j t)"),
-            )
+            nc.vector.quantize_mx(out=h_codes[b][:, cols].bitcast(FP8X4), scales=h_scales[b][:, cols], in_=grouped[:])
 
         out_rows = out.rearrange("(m p) j -> p m j", p=P)
 
-        def second_stage(h):
-            cols = slice(h * HALF, (h + 1) * HALF)
+        def second_stage(j0, width, shared):
+            cols = slice(j0, j0 + width)
             for pair in range(2):
-                acc = psum.tile([P, 2 * HALF], F32, name="bank")
+                acc = psum.tile([P, 2, width], F32, name="acc", bufs=2)
                 for b in range(H_PASSES):
                     for u in range(2):
                         m = 2 * pair + u
                         nc.tensor.matmul_mx(
-                            out=acc[:, u * HALF : (u + 1) * HALF],
+                            out=acc[:, u, :],
                             lhsT=w2_codes[b][:, m * P : (m + 1) * P].bitcast(FP8X4),
                             lhsT_scale=w2_scales[b][0][:, m * P : (m + 1) * P],
-                            rhs=h_codes[b, h][:].bitcast(FP8X4),
-                            rhs_scale=h_scales[b, h][:],
+                            rhs=h_codes[b][:, cols].bitcast(FP8X4),
+                            rhs_scale=h_scales[b][:, cols],
                             start=(b == 0 and u == 0),
                             stop=(b == H_PASSES - 1 and u == 1),
                         )
-                result = work.tile([P, 2, HALF], F32, name="result", bufs=4)
+                result = work.tile([P, 2, width], F32, name="result", bufs=4)
                 for u in range(2):
                     m = 2 * pair + u
-                    if h == 1 and pair == 1:
-                        nc.vector.tensor_scalar(
-                            result[:, u, :], acc[:, u * HALF : (u + 1) * HALF], bias[:, m : m + 1], None, ALU.add
-                        )
+                    if shared and pair == 1:
+                        nc.vector.tensor_scalar(result[:, u, :], acc[:, u, :], bias[:, m : m + 1], None, ALU.add)
                     else:
                         nc.scalar.activation(
-                            out=result[:, u, :],
-                            in_=acc[:, u * HALF : (u + 1) * HALF],
-                            func=ACT.Identity,
-                            bias=bias[:, m : m + 1],
+                            out=result[:, u, :], in_=acc[:, u, :], func=ACT.Identity, bias=bias[:, m : m + 1]
                         )
                 nc.sync.dma_start(out=out_rows[:, 2 * pair : 2 * pair + 2, cols], in_=result[:])
 
-        first_stage(0, 0)
-        first_stage(0, 1)
+        first_stage(0, 0, HALF)
+        first_stage(0, HALF, HALF)
         quantize_w2(0)
-        first_stage(1, 0)
+        first_stage(1, 0, HALF)
         quantize_w2(1)
-        second_stage(0)
-        first_stage(1, 1)
-        second_stage(1)
+        second_stage(0, HALF, False)
+        first_stage(1, HALF, HALF)
+        second_stage(HALF, HALF, True)

@@ -160,7 +160,27 @@ def tile_list_rumour_distortion_scores_kernel(
             h_codes.append(keep.tile([P, S], U32, name="h_codes%d" % b, align_bytes=64))
             h_scales.append(keep.tile([P, S], U8, name="h_scales%d" % b, align_bytes=64))
 
-        def first_stage(b, j0, width):
+        banks = {}
+
+        def first_stage_pass(b, j0, width, q, l, a):
+            per_bank = BANK // width
+            if a == 0:
+                banks[b, j0, q, l] = psum.tile([P, BANK], F32, name="bank")
+            bank = banks[b, j0, q, l]
+            for u in range(per_bank):
+                t = per_bank * q + u
+                w_col = W1_COL + b * K_PASS + t * P
+                nc.tensor.matmul_mx(
+                    out=bank[:, u * width : (u + 1) * width],
+                    lhsT=w1_codes[b][:, a, t, :].bitcast(FP4X4),
+                    lhsT_scale=planes[a][:, w_col : w_col + P],
+                    rhs=picked[l, a][:, j0 : j0 + width].bitcast(FP8X4),
+                    rhs_scale=planes[a][:, l * S + j0 : l * S + j0 + width],
+                    start=(a == 0 and u == 0),
+                    stop=(a == K_PASSES - 1 and u == per_bank - 1),
+                )
+
+        def first_stage(b, j0, width, last):
             cols = slice(j0, j0 + width)
             per_bank = BANK // width
             groups = PACK // per_bank
@@ -168,29 +188,21 @@ def tile_list_rumour_distortion_scores_kernel(
             for q in range(groups):
                 sums = {}
                 for l in LIST_ORDER:
-                    bank = psum.tile([P, BANK], F32, name="bank", bufs=6)
-                    for a in range(K_PASSES):
-                        for u in range(per_bank):
-                            t = per_bank * q + u
-                            w_col = W1_COL + b * K_PASS + t * P
-                            nc.tensor.matmul_mx(
-                                out=bank[:, u * width : (u + 1) * width],
-                                lhsT=w1_codes[b][:, a, t, :].bitcast(FP4X4),
-                                lhsT_scale=planes[a][:, w_col : w_col + P],
-                                rhs=picked[l, a][:, cols].bitcast(FP8X4),
-                                rhs_scale=planes[a][:, l * S + j0 : l * S + j0 + width],
-                                start=(a == 0 and u == 0),
-                                stop=(a == K_PASSES - 1 and u == per_bank - 1),
-                            )
-                    sums[l] = bank[:].rearrange("p (u j) -> p j u", u=per_bank)
+                    if (b, j0, q, l) not in banks:
+                        first_stage_pass(b, j0, width, q, l, 0)
+                    first_stage_pass(b, j0, width, q, l, 1)
+                    sums[l] = banks[b, j0, q, l][:].rearrange("p (u j) -> p j u", u=per_bank)
                 copy_sums = work.tile([P, width, per_bank], F32, name="copy_sums", bufs=3)
                 nc.scalar.copy(out=copy_sums[:], in_=sums[COPY])
                 diffs = work.tile([P, 2, width, per_bank], F32, name="diffs", bufs=3)
                 nc.vector.tensor_tensor(diffs[:, 0], sums[POST], copy_sums[:], ALU.subtract)
                 nc.vector.tensor_tensor(diffs[:, 1], sums[PRESS], copy_sums[:], ALU.subtract)
-                nc.scalar.activation(
-                    out=gaps[:, :, q, :], in_=diffs[:].rearrange("p d j u -> p d (j u)"), func=ACT.Abs
-                )
+                flat = diffs[:].rearrange("p d j u -> p d (j u)")
+                if last and q == groups - 1:
+                    for d in range(2):
+                        nc.scalar.activation(out=gaps[:, d, q, :], in_=flat[:, d, :], func=ACT.Abs)
+                else:
+                    nc.scalar.activation(out=gaps[:, :, q, :], in_=flat, func=ACT.Abs)
             grouped = work.tile([P, width * PACK], BF16, name="h_grouped", align_bytes=64)
             nc.vector.tensor_tensor(
                 grouped[:].rearrange("p (j q u) -> p j q u", q=groups, u=per_bank),
@@ -205,8 +217,9 @@ def tile_list_rumour_distortion_scores_kernel(
         def second_stage(j0, width, shared):
             cols = slice(j0, j0 + width)
             for pair in range(2):
-                acc = psum.tile([P, 2, width], F32, name="acc", bufs=2)
-                for b in range(H_PASSES):
+                acc = psum.tile([P, 2, width], F32, name="bank")
+                order = (0, 1)
+                for b in order:
                     for u in range(2):
                         m = 2 * pair + u
                         nc.tensor.matmul_mx(
@@ -215,8 +228,8 @@ def tile_list_rumour_distortion_scores_kernel(
                             lhsT_scale=w2_scales[b][0][:, m * P : (m + 1) * P],
                             rhs=h_codes[b][:, cols].bitcast(FP8X4),
                             rhs_scale=h_scales[b][:, cols],
-                            start=(b == 0 and u == 0),
-                            stop=(b == H_PASSES - 1 and u == 1),
+                            start=(b == order[0] and u == 0),
+                            stop=(b == order[1] and u == 1),
                         )
                 result = work.tile([P, 2, width], F32, name="result", bufs=4)
                 for u in range(2):
@@ -229,11 +242,16 @@ def tile_list_rumour_distortion_scores_kernel(
                         )
                 nc.sync.dma_start(out=out_rows[:, 2 * pair : 2 * pair + 2, cols], in_=result[:])
 
-        first_stage(0, 0, HALF)
-        first_stage(0, HALF, HALF)
+        early = [(j0, q, l) for j0 in (0, HALF) for q in range(2) for l in LIST_ORDER][:8]
+        for l in LIST_ORDER:
+            for j0, q, listed in early:
+                if listed == l:
+                    first_stage_pass(0, j0, HALF, q, l, 0)
+        first_stage(0, 0, HALF, False)
+        first_stage(0, HALF, HALF, False)
         quantize_w2(0)
-        first_stage(1, 0, HALF)
+        first_stage(1, 0, HALF, False)
         quantize_w2(1)
+        first_stage(1, HALF, HALF, True)
         second_stage(0, HALF, False)
-        first_stage(1, HALF, HALF)
         second_stage(HALF, HALF, True)

from contextlib import ExitStack

import concourse.mybir as mybir

K, H, N, T, S = 1024, 1024, 512, 4096, 512
FLOPS = 2 * (3 * K * H * S + H * N * S)

F32 = mybir.dt.float32
BF16 = mybir.dt.bfloat16
I32 = mybir.dt.int32
U32 = mybir.dt.uint32
U16 = mybir.dt.uint16
U8 = mybir.dt.uint8
FP8X4 = mybir.dt.float8_e4m3fn_x4
FP4X4 = mybir.dt.float4_e2m1fn_x4
ALU = mybir.AluOpType
ACT = mybir.ActivationFunctionType

P = 128
PACK = 4
K_PASS = P * PACK
K_PASSES = K // K_PASS
H_PASSES = H // K_PASS
RUN = 8
BLOCKS = K_PASS // 32
QUADS = 4
HALF = S // 2
W1_COL = 3 * S
BANK = 512
POST, COPY, PRESS = 0, 1, 2
LIST_ORDER = (COPY, POST, PRESS)


def tile_list_rumour_distortion_scores_kernel(
    tc, tab_words, tab_scales, w1_words, w1_scales, w2, b2, offs, offs2, offs3, out
):
    nc = tc.nc
    with ExitStack() as ctx:
        keep = ctx.enter_context(tc.tile_pool(name="keep", bufs=1))
        work = ctx.enter_context(tc.tile_pool(name="work", bufs=2))
        psum = ctx.enter_context(tc.psum_pool(name="psum", bufs=8))

        scale_window = keep.tile([P, T], U8, name="scale_window", align_bytes=64)
        nc.sync.dma_start(
            out=scale_window[0:32, :].bitcast(I32),
            in_=tab_scales.rearrange("a q t -> (a q) t").bitcast(I32),
        )
        nc.vector.memset(scale_window[32:64, :].bitcast(I32), 0)
        nc.vector.memset(scale_window[64:128, :].bitcast(I32), 0)

        w1_scale_raw = keep.tile([P, H], U8, name="w1_scale_raw", align_bytes=64)
        nc.sync.dma_start(
            out=w1_scale_raw[0:32, :].bitcast(I32),
            in_=w1_scales.rearrange("a q c -> (a q) c").bitcast(I32),
        )
        nc.gpsimd.memset(w1_scale_raw[32:64, :].bitcast(I32), 0)
        nc.gpsimd.memset(w1_scale_raw[64:128, :].bitcast(I32), 0)

        list_inputs = (offs, offs2, offs3)
        lists = {}
        for l in LIST_ORDER:
            lists[l] = keep.tile([P, S // 16], U16, name="list%d" % l)
            nc.sync.dma_start(lists[l][:], list_inputs[l])

        def load_table(a):
            window = keep.tile([P, T], U32, name="word_window%d" % a, tag="table%d" % a, align_bytes=64)
            nc.sync.dma_start(
                out=window[:].bitcast(I32),
                in_=tab_words[a].rearrange("p t i -> p (t i)").bitcast(I32),
            )
            return window

        def load_w1(b, tag):
            raw = keep.tile([P, K_PASSES, 2 * K_PASS], U8, name="w1_raw%d" % b, tag=tag, align_bytes=64)
            nc.sync.dma_start(
                out=raw[:].bitcast(I32),
                in_=w1_words[:, :, 2 * K_PASS * b : 2 * K_PASS * (b + 1)].rearrange("a p c -> p a c").bitcast(I32),
            )
            dealt = keep.tile([P, K_PASSES, PACK, 2 * P], U8, name="w1_dealt%d" % b, align_bytes=64)
            nc.scalar.copy(
                out=dealt[:].bitcast(U32).rearrange("p a t (g w) -> p a t g w", g=BLOCKS),
                in_=raw[:].bitcast(U32).rearrange("p a (g t w) -> p a t g w", g=BLOCKS, t=PACK),
            )
            return dealt

        word_windows = [load_table(0)]
        w1_codes = [load_w1(0, "w1_then_w2")]
        word_windows.append(load_table(1))

        planes = []
        for a in range(K_PASSES):
            planes.append(keep.tile([P, W1_COL + H], U8, name="plane%d" % a, align_bytes=64))
        nc.gpsimd.memset(planes[1][:].bitcast(I32), 0)
        nc.scalar.copy(
            out=planes[0][:, W1_COL:].bitcast(U32).rearrange("p (b t g w) -> p b t g w", t=PACK, g=BLOCKS, w=2),
            in_=w1_scale_raw[:].bitcast(U32).rearrange("p (b g t w) -> p b t g w", t=PACK, g=BLOCKS, w=2),
        )
        picked_scales = keep.tile([P, 3 * S], U8, name="picked_scales", align_bytes=64)
        for l in LIST_ORDER:
            nc.vector.tensor_copy(picked_scales[:, l * S : (l + 1) * S], scale_window[:].indirect(lists[l][:]))
        nc.vector.tensor_copy(planes[0][:, 0:W1_COL].bitcast(I32), picked_scales[:].bitcast(I32))
        for a in range(K_PASSES):
            for q in range(QUADS):
                if a + q > 0:
                    row = BLOCKS * a + 4 * q
                    nc.scalar.dma_start(
                        out=planes[a][32 * q : 32 * q + 4, :].bitcast(I32),
                        in_=planes[0][row : row + 4, :].bitcast(I32),
                    )

        picked = {}
        for a in range(K_PASSES):
            for l in LIST_ORDER:
                picked[l, a] = keep.tile([P, S], U32, name="picked%d_%d" % (l, a), align_bytes=64)
        for l in LIST_ORDER:
            nc.vector.tensor_copy(picked[l, 0][:], word_windows[0][:].indirect(lists[l][:]))
        for h in range(2):
            for l in LIST_ORDER:
                nc.vector.tensor_copy(
                    picked[l, 1][:, h * HALF : (h + 1) * HALF],
                    word_windows[1][:].indirect(lists[l][:, h * 16 : (h + 1) * 16]),
                )

        w1_codes.append(load_w1(1, "table0"))
        w2_raw = keep.tile([P, H_PASSES * PACK * N + N // P], F32, name="w2_raw", tag="w1_then_w2", align_bytes=64)
        bias = w2_raw[:, H_PASSES * PACK * N :]

        w2_codes = []
        w2_scales = []
        for b in range(H_PASSES):
            rows = w2[K_PASS * b : K_PASS * (b + 1), :].rearrange("(g t i) n -> t g i n", g=BLOCKS, t=PACK)
            raw = w2_raw[:, b * PACK * N : (b + 1) * PACK * N].rearrange("p (t n) -> p t n", t=PACK)
            for t in range(PACK):
                nc.sync.dma_start(out=raw[:, t, :], in_=rows[t])
            grouped = keep.tile([P, N, PACK], BF16, name="w2_grouped%d" % b, align_bytes=64)
            for m in range(N // P):
                cols = slice(m * P, (m + 1) * P)
                nc.gpsimd.tensor_scalar(
                    grouped[:, cols, :], raw[:, :, cols].rearrange("p t n -> p n t"), 1.0, 0.0, ALU.mult, ALU.add
                )
            codes = keep.tile([P, N], U32, name="w2_codes%d" % b, align_bytes=64)
            scales = keep.tile([P, N], U8, name="w2_scales%d" % b, align_bytes=64)
            w2_codes.append(codes)
            w2_scales.append((scales, grouped))

        with nc.allow_non_contiguous_dma(reason="one bias value a partition"):
            nc.sync.dma_start(out=bias, in_=b2.rearrange("(m p) -> p m", p=P))

        def quantize_w2(b):
            scales, grouped = w2_scales[b]
            nc.vector.quantize_mx(
                out=w2_codes[b][:].bitcast(FP8X4),
                scales=scales[:],
                in_=grouped[:].rearrange("p n t -> p (n t)"),
            )

        h_codes = []
        h_scales = []
        for b in range(H_PASSES):
            h_codes.append(keep.tile([P, S], U32, name="h_codes%d" % b, align_bytes=64))
            h_scales.append(keep.tile([P, S], U8, name="h_scales%d" % b, align_bytes=64))

        banks = {}

        def first_stage_pass(b, j0, width, q, l, a):
            per_bank = BANK // width
            if a == 0:
                banks[b, j0, q, l] = psum.tile([P, BANK], F32, name="bank")
            bank = banks[b, j0, q, l]
            for u in range(per_bank):
                t = per_bank * q + u
                w_col = W1_COL + b * K_PASS + t * P
                nc.tensor.matmul_mx(
                    out=bank[:, u * width : (u + 1) * width],
                    lhsT=w1_codes[b][:, a, t, :].bitcast(FP4X4),
                    lhsT_scale=planes[a][:, w_col : w_col + P],
                    rhs=picked[l, a][:, j0 : j0 + width].bitcast(FP8X4),
                    rhs_scale=planes[a][:, l * S + j0 : l * S + j0 + width],
                    start=(a == 0 and u == 0),
                    stop=(a == K_PASSES - 1 and u == per_bank - 1),
                )

        def first_stage(b, j0, width, last):
            cols = slice(j0, j0 + width)
            per_bank = BANK // width
            groups = PACK // per_bank
            gaps = work.tile([P, 2, groups, BANK], F32, name="gaps")
            for q in range(groups):
                sums = {}
                for l in LIST_ORDER:
                    if (b, j0, q, l) not in banks:
                        first_stage_pass(b, j0, width, q, l, 0)
                    first_stage_pass(b, j0, width, q, l, 1)
                    sums[l] = banks[b, j0, q, l][:].rearrange("p (u j) -> p j u", u=per_bank)
                copy_sums = work.tile([P, width, per_bank], F32, name="copy_sums", bufs=3)
                nc.scalar.copy(out=copy_sums[:], in_=sums[COPY])
                diffs = work.tile([P, 2, width, per_bank], F32, name="diffs", bufs=3)
                nc.vector.tensor_tensor(diffs[:, 0], sums[POST], copy_sums[:], ALU.subtract)
                nc.vector.tensor_tensor(diffs[:, 1], sums[PRESS], copy_sums[:], ALU.subtract)
                flat = diffs[:].rearrange("p d j u -> p d (j u)")
                if last and q == groups - 1:
                    for d in range(2):
                        nc.scalar.activation(out=gaps[:, d, q, :], in_=flat[:, d, :], func=ACT.Abs)
                else:
                    nc.scalar.activation(out=gaps[:, :, q, :], in_=flat, func=ACT.Abs)
            grouped = work.tile([P, width * PACK], BF16, name="h_grouped", align_bytes=64)
            nc.vector.tensor_tensor(
                grouped[:].rearrange("p (j q u) -> p j q u", q=groups, u=per_bank),
                gaps[:, 0].rearrange("p q (j u) -> p j q u", u=per_bank),
                gaps[:, 1].rearrange("p q (j u) -> p j q u", u=per_bank),
                ALU.max,
            )
            nc.vector.quantize_mx(out=h_codes[b][:, cols].bitcast(FP8X4), scales=h_scales[b][:, cols], in_=grouped[:])

        out_rows = out.rearrange("(m p) j -> p m j", p=P)

        def second_stage(j0, width, shared):
            cols = slice(j0, j0 + width)
            for pair in range(2):
                acc = psum.tile([P, 2, width], F32, name="bank")
                order = (0, 1)
                for b in order:
                    for u in range(2):
                        m = 2 * pair + u
                        nc.tensor.matmul_mx(
                            out=acc[:, u, :],
                            lhsT=w2_codes[b][:, m * P : (m + 1) * P].bitcast(FP8X4),
                            lhsT_scale=w2_scales[b][0][:, m * P : (m + 1) * P],
                            rhs=h_codes[b][:, cols].bitcast(FP8X4),
                            rhs_scale=h_scales[b][:, cols],
                            start=(b == order[0] and u == 0),
                            stop=(b == order[1] and u == 1),
                        )
                result = work.tile([P, 2, width], F32, name="result", bufs=4)
                for u in range(2):
                    m = 2 * pair + u
                    if shared and pair == 1:
                        nc.vector.tensor_scalar(result[:, u, :], acc[:, u, :], bias[:, m : m + 1], None, ALU.add)
                    else:
                        nc.scalar.activation(
                            out=result[:, u, :], in_=acc[:, u, :], func=ACT.Identity, bias=bias[:, m : m + 1]
                        )
                nc.sync.dma_start(out=out_rows[:, 2 * pair : 2 * pair + 2, cols], in_=result[:])

        early = [(j0, q, l) for j0 in (0, HALF) for q in range(2) for l in LIST_ORDER][:8]
        for l in LIST_ORDER:
            for j0, q, listed in early:
                if listed == l:
                    first_stage_pass(0, j0, HALF, q, l, 0)
        first_stage(0, 0, HALF, False)
        first_stage(0, HALF, HALF, False)
        quantize_w2(0)
        first_stage(1, 0, HALF, False)
        quantize_w2(1)
        first_stage(1, HALF, HALF, True)
        second_stage(0, HALF, False)
        second_stage(HALF, HALF, True)
